import numpy as np
import ml_dtypes


def mxq(x, axis, fmt="e4m3"):
    dtype, down = {"e4m3": (ml_dtypes.float8_e4m3fn, 7), "e5m2": (ml_dtypes.float8_e5m2, 14)}[fmt]
    v = np.moveaxis(np.asarray(x, np.float32).astype(ml_dtypes.bfloat16).astype(np.float64), axis, -1)
    blocks = v.reshape(v.shape[:-1] + (-1, 32))
    amax = np.abs(blocks).max(-1, keepdims=True)
    byte = np.maximum(np.where(amax > 0, np.frexp(amax)[1] - 1 + 127, 0) - down, 1)
    scale = np.exp2(byte - 127.0)
    codes = (blocks / scale).astype(np.float32).astype(dtype).astype(np.float64)
    return np.moveaxis((codes * scale).reshape(v.shape), -1, axis)


WIDE = False


def mx_kscale(k):
    if not WIDE:
        return np.ones(k)
    levels = np.array([10, -10, 5, -5, 0])
    if k % 512:
        return np.exp2(np.random.permutation(np.resize(levels, k // 32))).repeat(32)
    a = np.empty((k // 512, 16))
    for p in range(k // 512):
        a[p, :8] = np.random.permutation(np.resize(levels, 8))
        for g in range(8):
            far = levels[np.abs(levels - a[p, g]) >= 10]
            a[p, g + 8] = far[np.random.randint(len(far))]
    return np.exp2(a.ravel()).repeat(32)


def f64(x):
    return np.asarray(x).astype(np.float64)


def striped(idx):
    return np.tile(idx.reshape(-1, 16).T, (8, 1)).astype(np.uint16)


def unstriped(offs):
    return offs[:16].T.reshape(-1).astype(np.int64)


def pack_weight(w):
    k, n = w.shape
    w = f64(np.asarray(w, np.float32).astype(ml_dtypes.bfloat16)).reshape(k // 32, 32, n)
    amax = np.abs(w).max(1)
    byte = np.clip(np.where(amax > 0, np.frexp(amax)[1] - 1 + 127 - 7, 1), 1, 254)
    scaled = (w * np.exp2(127.0 - byte)[:, None, :]).reshape(k, n).astype(np.float32)
    words = np.ascontiguousarray(scaled.reshape(k // 512, 128, 4, n).transpose(0, 1, 3, 2)).astype(ml_dtypes.float8_e4m3fn).view(np.uint8)
    return words, np.ascontiguousarray(byte.astype(np.uint8).reshape(k // 512, 16, n))


def unpack_weight(words, scales):
    g, p, n, _ = words.shape
    vals = np.ascontiguousarray(words).view(ml_dtypes.float8_e4m3fn).astype(np.float64) * np.repeat(np.exp2(scales.astype(np.float64) - 127.0), 8, axis=1)[..., None]
    return vals.transpose(0, 1, 3, 2).reshape(g * 512, n)


K, T, S, N, V = 1024, 2048, 512, 128, 256


def setup_inputs():
    n = np.random.standard_normal
    s = mx_kscale(K)[:, None]
    packed_xT = pack_weight(n((K, T)) * s)
    return {
        "x_words": packed_xT[0],
        "x_scales": packed_xT[1],
        "w1": (n((K, N)) / np.sqrt(K) / s).astype(np.float32),
        "sharp": (np.random.uniform(0.8, 2.5, (N, 1))).astype(np.float32),
        "offs": striped(np.random.permutation(T)[:S]),
        "pos1": striped(np.random.permutation(S)[:V]),
        "pos2": striped(np.random.permutation(S)[:V]),
        "pos3": striped(np.random.permutation(S)[:V]),
        "pos4": striped(np.random.permutation(S)[:V]),
        "cen": striped(np.random.permutation(S)[:V]),
    }


def reference(x_words, x_scales, w1, sharp, offs, pos1, pos2, pos3, pos4, cen):
    xq = unpack_weight(x_words, x_scales)[:, unstriped(offs)]
    y = mxq(f64(w1), 0, "e4m3").T @ xq
    g0 = y[:, unstriped(pos1)]
    g1 = y[:, unstriped(pos2)]
    g2 = y[:, unstriped(pos3)]
    g3 = y[:, unstriped(pos4)]
    lo = np.maximum(np.minimum(g0, g1), np.minimum(g2, g3))
    hi = np.minimum(np.maximum(g0, g1), np.maximum(g2, g3))
    gc = y[:, unstriped(cen)]
    med = np.maximum(np.minimum(lo, hi), np.minimum(np.maximum(lo, hi), gc))
    dev = np.abs(gc - med)
    return med + (gc - med) * (np.exp(-1.0 * (f64(sharp) * dev)))

@@ -1,0 +1,136 @@
+from contextlib import ExitStack
+
+import concourse.mybir as mybir
+
+K, T, S, N, V = 1024, 2048, 512, 128, 256
+FLOPS = 2 * K * S * N
+
+F32 = mybir.dt.float32
+BF16 = mybir.dt.bfloat16
+U32 = mybir.dt.uint32
+I32 = mybir.dt.int32
+U16 = mybir.dt.uint16
+U8 = mybir.dt.uint8
+FP8X4 = mybir.dt.float8_e4m3fn_x4
+ALU = mybir.AluOpType
+ACT = mybir.ActivationFunctionType
+
+P = 128
+PASSES = 2
+
+
+def tile_picked_ymed5f_soft_p_kernel(tc, x_words, x_scales, w1, sharp, offs, pos1, pos2, pos3, pos4, cen, out):
+    nc = tc.nc
+    with ExitStack() as ctx:
+        keep = ctx.enter_context(tc.tile_pool(name="keep", bufs=1))
+        psum = ctx.enter_context(tc.psum_pool(name="psum", bufs=1))
+
+        scale_table = keep.tile([P, T], U8, name="scale_table", align_bytes=64)
+        nc.vector.memset(scale_table[:].bitcast(I32), 0)
+
+        warm = keep.tile([P, 8], F32, name="warm")
+        warm_out = keep.tile([P, 8], F32, name="warm_out")
+        nc.gpsimd.memset(warm[:], 0.0)
+        nc.scalar.activation(warm_out[:], warm[:], ACT.Exp)
+
+        w_raw = keep.tile([P, PASSES, 4 * N], F32, name="w_raw")
+        nc.sync.dma_start(w_raw[:], w1.rearrange("(g p j) m -> p g (j m)", g=PASSES, j=4))
+        offs_sb = keep.tile([P, S // 16], U16, name="offs_sb")
+        nc.sync.dma_start(offs_sb[:], offs)
+        for q in range(4):
+            nc.sync.dma_start(
+                scale_table[32 * q : 32 * q + 8, :].bitcast(I32),
+                x_scales[:, 4 * q : 4 * q + 4, :].bitcast(I32),
+            )
+        word_tables = []
+        for g in range(PASSES):
+            table = keep.tile([P, T], I32, name=f"word_table{g}")
+            nc.sync.dma_start(table[:], x_words[g].rearrange("p c r -> p (c r)").bitcast(I32))
+            word_tables.append(table)
+        lists = []
+        for name, src in (("pos1", pos1), ("pos2", pos2), ("pos3", pos3), ("pos4", pos4), ("cen", cen)):
+            held = keep.tile([P, V // 16], U16, name=f"{name}_sb")
+            nc.sync.dma_start(held[:], src)
+            lists.append(held)
+        sharp_sb = keep.tile([P, 1], F32, name="sharp_sb")
+        nc.sync.dma_start(sharp_sb[:], sharp)
+
+        neg_sharp = keep.tile([P, 1], F32, name="neg_sharp")
+        nc.scalar.activation(neg_sharp[:], sharp_sb[:], ACT.Copy, scale=-1.0)
+
+        w_bf = keep.tile([P, PASSES, N, 4], BF16, name="w_bf", align_bytes=64)
+        for g in range(PASSES):
+            nc.scalar.copy(w_bf[:, g, :, :], w_raw[:, g, :].rearrange("p (j m) -> p m j", j=4))
+        w_codes = keep.tile([P, PASSES * N], U32, name="w_codes", align_bytes=64)
+        w_scales = keep.tile([P, PASSES * N], U8, name="w_scales", align_bytes=64)
+
+        x_scale = keep.tile([P, S], U8, name="x_scale", align_bytes=64)
+        nc.vector.tensor_copy(x_scale[:], scale_table[:].indirect(offs_sb[:]))
+        nc.vector.quantize_mx(w_codes[:].bitcast(FP8X4), w_scales[:], w_bf[:].rearrange("p g m j -> p (g m j)"))
+
+        x_codes = [keep.tile([P, S], U32, name=f"x_codes{g}", align_bytes=64) for g in range(PASSES)]
+        nc.vector.tensor_copy(x_codes[0][:], word_tables[0][:].bitcast(U32).indirect(offs_sb[:]))
+        for h in range(2):
+            nc.vector.tensor_copy(
+                x_codes[1][:, 256 * h : 256 * h + 256],
+                word_tables[1][:].bitcast(U32).indirect(offs_sb[:, 16 * h : 16 * h + 16]),
+            )
+
+        spans = [(0, 256), (256, 384), (384, 512)]
+        banks = [psum.tile([P, 512], F32, name=f"bank{i}") for i in range(len(spans))]
+        for g in range(PASSES):
+            for (a, b), bank in zip(spans, banks):
+                nc.tensor.matmul_mx(
+                    bank[:, 0 : b - a],
+                    lhsT=w_codes[:, g * N : (g + 1) * N].bitcast(FP8X4),
+                    lhsT_scale=w_scales[:, g * N : (g + 1) * N],
+                    rhs=x_codes[g][:, a:b].bitcast(FP8X4),
+                    rhs_scale=x_scale[4 * g : P, a:b],
+                    start=(g == 0),
+                    stop=(g == PASSES - 1),
+                )
+        y = keep.tile([P, S], F32, name="y")
+        nc.scalar.copy(y[:, 0:256], banks[0][:, 0:256])
+        nc.scalar.copy(y[:, 256:384], banks[1][:, 0:128])
+        nc.vector.tensor_copy(y[:, 384:512], banks[2][:, 0:128])
+
+        def fresh(name, width=V):
+            return keep.tile([P, width], F32, name=name)
+
+        g0, g1, g2, g3, gc = [fresh(f"g{i}") for i in range(5)]
+        mn0, mx0, mn1, mx1, lo, hi, dlo, dhi = [fresh(n) for n in ("mn0", "mx0", "mn1", "mx1", "lo", "hi", "dlo", "dhi")]
+        nc.vector.tensor_copy(g0[:], y[:].indirect(lists[0][:]))
+        nc.vector.tensor_copy(g1[:], y[:].indirect(lists[1][:]))
+        nc.vector.tensor_copy(g2[:], y[:].indirect(lists[2][:]))
+        nc.vector.tensor_copy(g3[:], y[:].indirect(lists[3][:]))
+        nc.vector.tensor_copy(gc[:], y[:].indirect(lists[4][:]))
+        nc.vector.tensor_tensor(mn0[:], g0[:], g1[:], ALU.min)
+        nc.vector.tensor_tensor(mx0[:], g0[:], g1[:], ALU.max)
+        nc.vector.tensor_tensor(mn1[:], g2[:], g3[:], ALU.min)
+        nc.vector.tensor_tensor(mx1[:], g2[:], g3[:], ALU.max)
+        nc.vector.tensor_tensor(lo[:], mn0[:], mn1[:], ALU.max)
+        nc.vector.tensor_tensor(hi[:], mx0[:], mx1[:], ALU.min)
+        nc.vector.tensor_tensor(dlo[:], lo[:], gc[:], ALU.subtract)
+        nc.vector.tensor_tensor(dhi[:], hi[:], gc[:], ALU.subtract)
+
+        halves = [slice(0, 128), slice(128, 256)]
+        u = [fresh(f"u{h}", 128) for h in range(2)]
+        e = [fresh(f"e{h}", 128) for h in range(2)]
+        a = [fresh(f"a{h}", 128) for h in range(2)]
+        ex = [fresh(f"ex{h}", 128) for h in range(2)]
+        t = [fresh(f"t{h}", 128) for h in range(2)]
+        res = [fresh(f"res{h}", 128) for h in range(2)]
+        for h, c in enumerate(halves):
+            nc.vector.scalar_tensor_tensor(u[h][:], dlo[:, c], 0.0, dhi[:, c], ALU.max, ALU.min)
+        for h, c in enumerate(halves):
+            nc.vector.scalar_tensor_tensor(e[h][:], dlo[:, c], 0.0, u[h][:], ALU.min, ALU.max)
+        for h, c in enumerate(halves):
+            nc.scalar.activation(a[h][:], e[h][:], ACT.Abs)
+        for h, c in enumerate(halves):
+            nc.scalar.activation(ex[h][:], a[h][:], ACT.Exp, scale=neg_sharp[:])
+        for h, c in enumerate(halves):
+            nc.vector.scalar_tensor_tensor(t[h][:], ex[h][:], 1.0, e[h][:], ALU.subtract, ALU.mult)
+        for h, c in enumerate(halves):
+            nc.vector.tensor_tensor(res[h][:], gc[:, c], t[h][:], ALU.subtract)
+        nc.sync.dma_start(out[:, halves[0]], res[0][:])
+        nc.scalar.dma_start(out[:, halves[1]], res[1][:])

@@ -97,40 +97,43 @@ def tile_picked_ymed5f_soft_p_kernel(tc, x_words, x_scales, w1, sharp, offs, pos
         def fresh(name, width=V):
             return keep.tile([P, width], F32, name=name)
 
-        g0, g1, g2, g3, gc = [fresh(f"g{i}") for i in range(5)]
-        mn0, mx0, mn1, mx1, lo, hi, dlo, dhi = [fresh(n) for n in ("mn0", "mx0", "mn1", "mx1", "lo", "hi", "dlo", "dhi")]
-        nc.vector.tensor_copy(g0[:], y[:].indirect(lists[0][:]))
-        nc.vector.tensor_copy(g1[:], y[:].indirect(lists[1][:]))
-        nc.vector.tensor_copy(g2[:], y[:].indirect(lists[2][:]))
-        nc.vector.tensor_copy(g3[:], y[:].indirect(lists[3][:]))
-        nc.vector.tensor_copy(gc[:], y[:].indirect(lists[4][:]))
-        nc.vector.tensor_tensor(mn0[:], g0[:], g1[:], ALU.min)
-        nc.vector.tensor_tensor(mx0[:], g0[:], g1[:], ALU.max)
-        nc.vector.tensor_tensor(mn1[:], g2[:], g3[:], ALU.min)
-        nc.vector.tensor_tensor(mx1[:], g2[:], g3[:], ALU.max)
-        nc.vector.tensor_tensor(lo[:], mn0[:], mn1[:], ALU.max)
-        nc.vector.tensor_tensor(hi[:], mx0[:], mx1[:], ALU.min)
-        nc.vector.tensor_tensor(dlo[:], lo[:], gc[:], ALU.subtract)
-        nc.vector.tensor_tensor(dhi[:], hi[:], gc[:], ALU.subtract)
+        gc, d0, d1, d2, d3 = [fresh(n) for n in ("gc", "d0", "d1", "d2", "d3")]
+        m, big, lo, hi, a, b = [fresh(n) for n in ("m", "big", "lo", "hi", "a", "b")]
+        for h in range(2):
+            nc.vector.tensor_copy(gc[:, 128 * h : 128 * h + 128], y[:].indirect(lists[4][:, 8 * h : 8 * h + 8]))
+        for h in range(2):
+            c = slice(128 * h, 128 * h + 128)
+            d0h = d0[:, c]
+            nc.vector.tensor_tensor(d0h, y[:].indirect(lists[0][:, 8 * h : 8 * h + 8]), gc[:, c], ALU.subtract)
+        nc.vector.tensor_tensor(d1[:], y[:].indirect(lists[1][:]), gc[:], ALU.subtract)
+        nc.vector.tensor_tensor(d2[:], y[:].indirect(lists[2][:]), gc[:], ALU.subtract)
+        nc.vector.tensor_tensor(m[:], d0[:], d1[:], ALU.min)
+        nc.vector.tensor_tensor(big[:], d0[:], d1[:], ALU.max)
+        nc.vector.scalar_tensor_tensor(lo[:], d2[:], 0.0, m[:], ALU.min, ALU.max)
+        nc.vector.scalar_tensor_tensor(hi[:], d2[:], 0.0, big[:], ALU.max, ALU.min)
+        nc.vector.tensor_tensor(d3[:], y[:].indirect(lists[3][:]), gc[:], ALU.subtract)
+        nc.vector.tensor_tensor(b[:], lo[:], hi[:], ALU.max)
+        nc.vector.tensor_tensor(a[:], lo[:], hi[:], ALU.min)
 
-        halves = [slice(0, 128), slice(128, 256)]
-        u = [fresh(f"u{h}", 128) for h in range(2)]
-        e = [fresh(f"e{h}", 128) for h in range(2)]
-        a = [fresh(f"a{h}", 128) for h in range(2)]
-        ex = [fresh(f"ex{h}", 128) for h in range(2)]
-        t = [fresh(f"t{h}", 128) for h in range(2)]
-        res = [fresh(f"res{h}", 128) for h in range(2)]
-        for h, c in enumerate(halves):
-            nc.vector.scalar_tensor_tensor(u[h][:], dlo[:, c], 0.0, dhi[:, c], ALU.max, ALU.min)
-        for h, c in enumerate(halves):
-            nc.vector.scalar_tensor_tensor(e[h][:], dlo[:, c], 0.0, u[h][:], ALU.min, ALU.max)
-        for h, c in enumerate(halves):
-            nc.scalar.activation(a[h][:], e[h][:], ACT.Abs)
-        for h, c in enumerate(halves):
-            nc.scalar.activation(ex[h][:], a[h][:], ACT.Exp, scale=neg_sharp[:])
-        for h, c in enumerate(halves):
-            nc.vector.scalar_tensor_tensor(t[h][:], ex[h][:], 1.0, e[h][:], ALU.subtract, ALU.mult)
-        for h, c in enumerate(halves):
-            nc.vector.tensor_tensor(res[h][:], gc[:, c], t[h][:], ALU.subtract)
-        nc.sync.dma_start(out[:, halves[0]], res[0][:])
-        nc.scalar.dma_start(out[:, halves[1]], res[1][:])
+        PIECES = 4
+        W = V // PIECES
+        cols = [slice(W * h, W * h + W) for h in range(PIECES)]
+        u, e, mag, ex, t = [fresh(n) for n in ("u", "e", "mag", "ex", "t")]
+        STORES = 2
+        SW = V // STORES
+        res = [fresh(f"res{h}", SW) for h in range(STORES)]
+        for c in cols:
+            nc.vector.tensor_tensor(u[:, c], b[:, c], d3[:, c], ALU.min)
+        for c in cols:
+            nc.vector.tensor_tensor(e[:, c], a[:, c], u[:, c], ALU.max)
+        for c in cols:
+            nc.scalar.activation(mag[:, c], e[:, c], ACT.Abs)
+        for c in cols:
+            nc.scalar.activation(ex[:, c], mag[:, c], ACT.Exp, scale=neg_sharp[:])
+        for c in cols:
+            nc.vector.scalar_tensor_tensor(t[:, c], ex[:, c], 1.0, e[:, c], ALU.subtract, ALU.mult)
+        for c in cols:
+            s = c.start // SW
+            nc.vector.tensor_tensor(res[s][:, c.start - s * SW : c.stop - s * SW], gc[:, c], t[:, c], ALU.subtract)
+        for s in range(STORES):
+            (nc.sync if s % 2 == 0 else nc.scalar).dma_start(out[:, s * SW : (s + 1) * SW], res[s][:])

@@ -27,45 +27,51 @@ def tile_picked_ymed5f_soft_p_kernel(tc, x_words, x_scales, w1, sharp, offs, pos
 
         scale_table = keep.tile([P, T], U8, name="scale_table", align_bytes=64)
         nc.vector.memset(scale_table[:].bitcast(I32), 0)
+        x_scale = keep.tile([P, PASSES * S], U8, name="x_scale", align_bytes=64)
+        nc.vector.memset(x_scale[:].bitcast(I32), 0)
+
+        w_rows = w1.rearrange("(g p j) m -> g p (j m)", g=PASSES, j=4)
+        w_raw = [keep.tile([P, 4 * N], F32, name=f"w_raw{g}") for g in range(PASSES)]
+        nc.sync.dma_start(w_raw[0][:], w_rows[0])
 
         warm = keep.tile([P, 8], F32, name="warm")
         warm_out = keep.tile([P, 8], F32, name="warm_out")
         nc.gpsimd.memset(warm[:], 0.0)
         nc.scalar.activation(warm_out[:], warm[:], ACT.Exp)
 
-        w_raw = keep.tile([P, PASSES, 4 * N], F32, name="w_raw")
-        nc.sync.dma_start(w_raw[:], w1.rearrange("(g p j) m -> p g (j m)", g=PASSES, j=4))
-        offs_sb = keep.tile([P, S // 16], U16, name="offs_sb")
-        nc.sync.dma_start(offs_sb[:], offs)
-        for q in range(4):
-            nc.sync.dma_start(
-                scale_table[32 * q : 32 * q + 8, :].bitcast(I32),
-                x_scales[:, 4 * q : 4 * q + 4, :].bitcast(I32),
-            )
+        def load_list(name, src):
+            held = keep.tile([P, src.shape[1]], U16, name=f"{name}_sb")
+            nc.sync.dma_start(held[:], src)
+            return held
+
+        offs_sb = load_list("offs", offs)
+        nc.sync.dma_start(scale_table[0:P:4, :].bitcast(I32), x_scales.rearrange("g b c -> b g c").bitcast(I32))
+        nc.sync.dma_start(w_raw[1][:], w_rows[1])
         word_tables = []
         for g in range(PASSES):
             table = keep.tile([P, T], I32, name=f"word_table{g}")
             nc.sync.dma_start(table[:], x_words[g].rearrange("p c r -> p (c r)").bitcast(I32))
             word_tables.append(table)
-        lists = []
-        for name, src in (("pos1", pos1), ("pos2", pos2), ("pos3", pos3), ("pos4", pos4), ("cen", cen)):
-            held = keep.tile([P, V // 16], U16, name=f"{name}_sb")
-            nc.sync.dma_start(held[:], src)
-            lists.append(held)
+        lists = [load_list("pos1", pos1), load_list("pos2", pos2)]
+        cen_sb = load_list("cen", cen)
+        lists = lists + [load_list("pos3", pos3), load_list("pos4", pos4), cen_sb]
         sharp_sb = keep.tile([P, 1], F32, name="sharp_sb")
-        nc.sync.dma_start(sharp_sb[:], sharp)
+        nc.gpsimd.dma_start(sharp_sb[:], sharp)
 
-        neg_sharp = keep.tile([P, 1], F32, name="neg_sharp")
-        nc.scalar.activation(neg_sharp[:], sharp_sb[:], ACT.Copy, scale=-1.0)
+        picked_scales = keep.tile([P, S], U8, name="picked_scales", align_bytes=64)
+        nc.vector.tensor_copy(picked_scales[:], scale_table[:].indirect(offs_sb[:]))
+        for q in range(4):
+            nc.scalar.dma_start(
+                x_scale[32 * q : 32 * q + 4, :].bitcast(I32).rearrange("p (g s) -> p g s", g=PASSES),
+                picked_scales[32 * q : 32 * q + 32 : 4, :].bitcast(I32),
+            )
 
         w_bf = keep.tile([P, PASSES, N, 4], BF16, name="w_bf", align_bytes=64)
         for g in range(PASSES):
-            nc.scalar.copy(w_bf[:, g, :, :], w_raw[:, g, :].rearrange("p (j m) -> p m j", j=4))
+            nc.scalar.copy(w_bf[:, g, :, :], w_raw[g][:].rearrange("p (j m) -> p m j", j=4))
         w_codes = keep.tile([P, PASSES * N], U32, name="w_codes", align_bytes=64)
         w_scales = keep.tile([P, PASSES * N], U8, name="w_scales", align_bytes=64)
 
-        x_scale = keep.tile([P, S], U8, name="x_scale", align_bytes=64)
-        nc.vector.tensor_copy(x_scale[:], scale_table[:].indirect(offs_sb[:]))
         nc.vector.quantize_mx(w_codes[:].bitcast(FP8X4), w_scales[:], w_bf[:].rearrange("p g m j -> p (g m j)"))
 
         x_codes = [keep.tile([P, S], U32, name=f"x_codes{g}", align_bytes=64) for g in range(PASSES)]
@@ -85,7 +91,7 @@ def tile_picked_ymed5f_soft_p_kernel(tc, x_words, x_scales, w1, sharp, offs, pos
                     lhsT=w_codes[:, g * N : (g + 1) * N].bitcast(FP8X4),
                     lhsT_scale=w_scales[:, g * N : (g + 1) * N],
                     rhs=x_codes[g][:, a:b].bitcast(FP8X4),
-                    rhs_scale=x_scale[4 * g : P, a:b],
+                    rhs_scale=x_scale[:, g * S + a : g * S + b],
                     start=(g == 0),
                     stop=(g == PASSES - 1),
                 )
@@ -127,9 +133,9 @@ def tile_picked_ymed5f_soft_p_kernel(tc, x_words, x_scales, w1, sharp, offs, pos
         for c in cols:
             nc.vector.tensor_tensor(e[:, c], a[:, c], u[:, c], ALU.max)
         for c in cols:
-            nc.scalar.activation(mag[:, c], e[:, c], ACT.Abs)
+            nc.vector.scalar_tensor_tensor(mag[:, c], e[:, c], -1.0, e[:, c], ALU.mult, ALU.min)
         for c in cols:
-            nc.scalar.activation(ex[:, c], mag[:, c], ACT.Exp, scale=neg_sharp[:])
+            nc.scalar.activation(ex[:, c], mag[:, c], ACT.Exp, scale=sharp_sb[:])
         for c in cols:
             nc.vector.scalar_tensor_tensor(t[:, c], ex[:, c], 1.0, e[:, c], ALU.subtract, ALU.mult)
         for c in cols:

@@ -33,6 +33,7 @@ def tile_picked_ymed5f_soft_p_kernel(tc, x_words, x_scales, w1, sharp, offs, pos
         w_rows = w1.rearrange("(g p j) m -> g p (j m)", g=PASSES, j=4)
         w_raw = [keep.tile([P, 4 * N], F32, name=f"w_raw{g}") for g in range(PASSES)]
         nc.sync.dma_start(w_raw[0][:], w_rows[0])
+        nc.scalar.dma_start(w_raw[1][:], w_rows[1])
 
         warm = keep.tile([P, 8], F32, name="warm")
         warm_out = keep.tile([P, 8], F32, name="warm_out")
@@ -46,7 +47,6 @@ def tile_picked_ymed5f_soft_p_kernel(tc, x_words, x_scales, w1, sharp, offs, pos
 
         offs_sb = load_list("offs", offs)
         nc.sync.dma_start(scale_table[0:P:4, :].bitcast(I32), x_scales.rearrange("g b c -> b g c").bitcast(I32))
-        nc.sync.dma_start(w_raw[1][:], w_rows[1])
         word_tables = []
         for g in range(PASSES):
             table = keep.tile([P, T], I32, name=f"word_table{g}")
@@ -56,7 +56,7 @@ def tile_picked_ymed5f_soft_p_kernel(tc, x_words, x_scales, w1, sharp, offs, pos
         cen_sb = load_list("cen", cen)
         lists = lists + [load_list("pos3", pos3), load_list("pos4", pos4), cen_sb]
         sharp_sb = keep.tile([P, 1], F32, name="sharp_sb")
-        nc.gpsimd.dma_start(sharp_sb[:], sharp)
+        nc.sync.dma_start(sharp_sb[:], sharp)
 
         picked_scales = keep.tile([P, S], U8, name="picked_scales", align_bytes=64)
         nc.vector.tensor_copy(picked_scales[:], scale_table[:].indirect(offs_sb[:]))

from contextlib import ExitStack

import concourse.mybir as mybir

K, T, S, N, V = 1024, 2048, 512, 128, 256
FLOPS = 2 * K * S * N

F32 = mybir.dt.float32
BF16 = mybir.dt.bfloat16
U32 = mybir.dt.uint32
I32 = mybir.dt.int32
U16 = mybir.dt.uint16
U8 = mybir.dt.uint8
FP8X4 = mybir.dt.float8_e4m3fn_x4
ALU = mybir.AluOpType
ACT = mybir.ActivationFunctionType

P = 128
PASSES = 2


def tile_picked_ymed5f_soft_p_kernel(tc, x_words, x_scales, w1, sharp, offs, pos1, pos2, pos3, pos4, cen, out):
    nc = tc.nc
    with ExitStack() as ctx:
        keep = ctx.enter_context(tc.tile_pool(name="keep", bufs=1))
        psum = ctx.enter_context(tc.psum_pool(name="psum", bufs=1))

        scale_table = keep.tile([P, T], U8, name="scale_table", align_bytes=64)
        nc.vector.memset(scale_table[:].bitcast(I32), 0)
        x_scale = keep.tile([P, PASSES * S], U8, name="x_scale", align_bytes=64)
        nc.vector.memset(x_scale[:].bitcast(I32), 0)

        w_rows = w1.rearrange("(g p j) m -> g p (j m)", g=PASSES, j=4)
        w_raw = [keep.tile([P, 4 * N], F32, name=f"w_raw{g}") for g in range(PASSES)]
        nc.sync.dma_start(w_raw[0][:], w_rows[0])
        nc.scalar.dma_start(w_raw[1][:], w_rows[1])

        warm = keep.tile([P, 8], F32, name="warm")
        warm_out = keep.tile([P, 8], F32, name="warm_out")
        nc.gpsimd.memset(warm[:], 0.0)
        nc.scalar.activation(warm_out[:], warm[:], ACT.Exp)

        def load_list(name, src):
            held = keep.tile([P, src.shape[1]], U16, name=f"{name}_sb")
            nc.sync.dma_start(held[:], src)
            return held

        offs_sb = load_list("offs", offs)
        nc.sync.dma_start(scale_table[0:P:4, :].bitcast(I32), x_scales.rearrange("g b c -> b g c").bitcast(I32))
        word_tables = []
        for g in range(PASSES):
            table = keep.tile([P, T], I32, name=f"word_table{g}")
            nc.sync.dma_start(table[:], x_words[g].rearrange("p c r -> p (c r)").bitcast(I32))
            word_tables.append(table)
        lists = [load_list("pos1", pos1), load_list("pos2", pos2)]
        cen_sb = load_list("cen", cen)
        lists = lists + [load_list("pos3", pos3), load_list("pos4", pos4), cen_sb]
        sharp_sb = keep.tile([P, 1], F32, name="sharp_sb")
        nc.sync.dma_start(sharp_sb[:], sharp)

        picked_scales = keep.tile([P, S], U8, name="picked_scales", align_bytes=64)
        nc.vector.tensor_copy(picked_scales[:], scale_table[:].indirect(offs_sb[:]))
        for q in range(4):
            nc.scalar.dma_start(
                x_scale[32 * q : 32 * q + 4, :].bitcast(I32).rearrange("p (g s) -> p g s", g=PASSES),
                picked_scales[32 * q : 32 * q + 32 : 4, :].bitcast(I32),
            )

        w_bf = keep.tile([P, PASSES, N, 4], BF16, name="w_bf", align_bytes=64)
        for g in range(PASSES):
            nc.scalar.copy(w_bf[:, g, :, :], w_raw[g][:].rearrange("p (j m) -> p m j", j=4))
        w_codes = keep.tile([P, PASSES * N], U32, name="w_codes", align_bytes=64)
        w_scales = keep.tile([P, PASSES * N], U8, name="w_scales", align_bytes=64)

        nc.vector.quantize_mx(w_codes[:].bitcast(FP8X4), w_scales[:], w_bf[:].rearrange("p g m j -> p (g m j)"))

        x_codes = [keep.tile([P, S], U32, name=f"x_codes{g}", align_bytes=64) for g in range(PASSES)]
        nc.vector.tensor_copy(x_codes[0][:], word_tables[0][:].bitcast(U32).indirect(offs_sb[:]))
        for h in range(2):
            nc.vector.tensor_copy(
                x_codes[1][:, 256 * h : 256 * h + 256],
                word_tables[1][:].bitcast(U32).indirect(offs_sb[:, 16 * h : 16 * h + 16]),
            )

        spans = [(0, 256), (256, 384), (384, 512)]
        banks = [psum.tile([P, 512], F32, name=f"bank{i}") for i in range(len(spans))]
        for g in range(PASSES):
            for (a, b), bank in zip(spans, banks):
                nc.tensor.matmul_mx(
                    bank[:, 0 : b - a],
                    lhsT=w_codes[:, g * N : (g + 1) * N].bitcast(FP8X4),
                    lhsT_scale=w_scales[:, g * N : (g + 1) * N],
                    rhs=x_codes[g][:, a:b].bitcast(FP8X4),
                    rhs_scale=x_scale[:, g * S + a : g * S + b],
                    start=(g == 0),
                    stop=(g == PASSES - 1),
                )
        y = keep.tile([P, S], F32, name="y")
        nc.scalar.copy(y[:, 0:256], banks[0][:, 0:256])
        nc.scalar.copy(y[:, 256:384], banks[1][:, 0:128])
        nc.vector.tensor_copy(y[:, 384:512], banks[2][:, 0:128])

        def fresh(name, width=V):
            return keep.tile([P, width], F32, name=name)

        gc, d0, d1, d2, d3 = [fresh(n) for n in ("gc", "d0", "d1", "d2", "d3")]
        m, big, lo, hi, a, b = [fresh(n) for n in ("m", "big", "lo", "hi", "a", "b")]
        for h in range(2):
            nc.vector.tensor_copy(gc[:, 128 * h : 128 * h + 128], y[:].indirect(lists[4][:, 8 * h : 8 * h + 8]))
        for h in range(2):
            c = slice(128 * h, 128 * h + 128)
            d0h = d0[:, c]
            nc.vector.tensor_tensor(d0h, y[:].indirect(lists[0][:, 8 * h : 8 * h + 8]), gc[:, c], ALU.subtract)
        nc.vector.tensor_tensor(d1[:], y[:].indirect(lists[1][:]), gc[:], ALU.subtract)
        nc.vector.tensor_tensor(d2[:], y[:].indirect(lists[2][:]), gc[:], ALU.subtract)
        nc.vector.tensor_tensor(m[:], d0[:], d1[:], ALU.min)
        nc.vector.tensor_tensor(big[:], d0[:], d1[:], ALU.max)
        nc.vector.scalar_tensor_tensor(lo[:], d2[:], 0.0, m[:], ALU.min, ALU.max)
        nc.vector.scalar_tensor_tensor(hi[:], d2[:], 0.0, big[:], ALU.max, ALU.min)
        nc.vector.tensor_tensor(d3[:], y[:].indirect(lists[3][:]), gc[:], ALU.subtract)
        nc.vector.tensor_tensor(b[:], lo[:], hi[:], ALU.max)
        nc.vector.tensor_tensor(a[:], lo[:], hi[:], ALU.min)

        PIECES = 4
        W = V // PIECES
        cols = [slice(W * h, W * h + W) for h in range(PIECES)]
        u, e, mag, ex, t = [fresh(n) for n in ("u", "e", "mag", "ex", "t")]
        STORES = 2
        SW = V // STORES
        res = [fresh(f"res{h}", SW) for h in range(STORES)]
        for c in cols:
            nc.vector.tensor_tensor(u[:, c], b[:, c], d3[:, c], ALU.min)
        for c in cols:
            nc.vector.tensor_tensor(e[:, c], a[:, c], u[:, c], ALU.max)
        for c in cols:
            nc.vector.scalar_tensor_tensor(mag[:, c], e[:, c], -1.0, e[:, c], ALU.mult, ALU.min)
        for c in cols:
            nc.scalar.activation(ex[:, c], mag[:, c], ACT.Exp, scale=sharp_sb[:])
        for c in cols:
            nc.vector.scalar_tensor_tensor(t[:, c], ex[:, c], 1.0, e[:, c], ALU.subtract, ALU.mult)
        for c in cols:
            s = c.start // SW
            nc.vector.tensor_tensor(res[s][:, c.start - s * SW : c.stop - s * SW], gc[:, c], t[:, c], ALU.subtract)
        for s in range(STORES):
            (nc.sync if s % 2 == 0 else nc.scalar).dma_start(out[:, s * SW : (s + 1) * SW], res[s][:])
